import numpy as np
import ml_dtypes


def mxq(x, axis, fmt="e4m3"):
    dtype, down = {"e4m3": (ml_dtypes.float8_e4m3fn, 7), "e5m2": (ml_dtypes.float8_e5m2, 14)}[fmt]
    v = np.moveaxis(np.asarray(x, np.float32).astype(ml_dtypes.bfloat16).astype(np.float64), axis, -1)
    blocks = v.reshape(v.shape[:-1] + (-1, 32))
    amax = np.abs(blocks).max(-1, keepdims=True)
    byte = np.maximum(np.where(amax > 0, np.frexp(amax)[1] - 1 + 127, 0) - down, 1)
    scale = np.exp2(byte - 127.0)
    codes = (blocks / scale).astype(np.float32).astype(dtype).astype(np.float64)
    return np.moveaxis((codes * scale).reshape(v.shape), -1, axis)


WIDE = False


def mx_kscale(k):
    if not WIDE:
        return np.ones(k)
    levels = np.array([30, -30])
    if k % 512:
        return np.exp2(np.random.permutation(np.resize(levels, k // 32))).repeat(32)
    a = np.empty((k // 512, 16))
    for p in range(k // 512):
        a[p, :8] = np.random.permutation(np.resize(levels, 8))
        for g in range(8):
            far = levels[np.abs(levels - a[p, g]) >= 10]
            a[p, g + 8] = far[np.random.randint(len(far))]
    return np.exp2(a.ravel()).repeat(32)


BF16 = ml_dtypes.bfloat16


def bf(x):
    return np.asarray(x, np.float32).astype(BF16)


def f64(x):
    return np.asarray(x).astype(np.float64)


M, Q, N, K = 2048, 512, 1024, 1024


def setup_inputs():
    s = mx_kscale(Q)
    t = mx_kscale(N)
    u = mx_kscale(M)
    tail = np.exp(0.5 * np.random.standard_normal((N, Q)))
    return {"v": bf(np.random.standard_normal((M, Q)) * s),
            "e": bf(np.random.standard_normal((N, Q)) * tail / np.sqrt(Q) / s),
            "mean_grad": bf(0.4 * np.random.standard_normal(N)),
            "gate": bf(np.random.uniform(0.2, 1.5, (M, N)) * t * u[:, None]),
            "w": bf(np.random.standard_normal((K, N)) / np.sqrt(N) / t),
            "x": bf(np.random.standard_normal((M, K)) / np.sqrt(M) / u[:, None])}


def reference(v, e, mean_grad, gate, w, x):
    dz = mxq(f64(v), 1, "e4m3") @ mxq(f64(e), 1, "e5m2").T
    dh = (dz + f64(mean_grad)) * f64(gate)
    dx = mxq(dh, 1, "e5m2") @ mxq(f64(w), 1, "e4m3").T
    dw = mxq(f64(x), 0, "e4m3").T @ mxq(dh, 0, "e5m2")
    return dx, dw

@@ -1,0 +1,280 @@
+from contextlib import ExitStack
+
+import concourse.mybir as mybir
+from concourse.masks import make_identity
+
+M, Q, N, K = 2048, 512, 1024, 1024
+FLOPS = 2 * M * N * Q + 2 * M * K * N + 2 * K * N * M
+
+F32 = mybir.dt.float32
+BF16 = mybir.dt.bfloat16
+U32 = mybir.dt.uint32
+U8 = mybir.dt.uint8
+E4M3 = mybir.dt.float8_e4m3fn_x4
+E5M2 = mybir.dt.float8_e5m2_x4
+ADD = mybir.AluOpType.add
+MULT = mybir.AluOpType.mult
+
+P = 128
+PACK = 4
+G = P * PACK
+TILES = [(i, g) for i in range(4) for g in range(2)]
+
+
+def tile_cross_moment_backward_s6_kernel(tc, v, e, mean_grad, gate, w, x, dx, dw):
+    nc = tc.nc
+    with ExitStack() as ctx:
+        keep = ctx.enter_context(tc.tile_pool(name="keep", bufs=1))
+        work = ctx.enter_context(tc.tile_pool(name="work", bufs=2))
+        psum = ctx.enter_context(tc.psum_pool(name="psum", bufs=2))
+        ctx.enter_context(tc.manual_schedule())
+
+        ident = keep.tile([P, P], F32, name="ident")
+        make_identity(nc, ident[:])
+
+        raw = {}
+        packed = {}
+        mx = {}
+        banks = {}
+        dz = {}
+        dh = {}
+
+        def load(key, src, tag, bufs):
+            tile = work.tile(list(src.shape), BF16, name=tag, tag=tag, bufs=bufs)
+            nc.sync.dma_start(out=tile[:], in_=src)
+            raw[key] = tile
+
+        def rows4(src, i):
+            return src[i * G : (i + 1) * G, :].rearrange("(c t) f -> c t f", t=PACK)
+
+        def rows2(src, i):
+            return src[i * G : (i + 1) * G, :].rearrange("(h c u) f -> c h u f", h=2, u=2)
+
+        def load_e(g):
+            load(("e", g), rows4(e, g), "rows", 6)
+
+        def load_v(i):
+            load(("v", i), rows2(v, i), "rows", 6)
+
+        def load_w(g, h):
+            src = w[h * G : (h + 1) * G, g * G : (g + 1) * G].rearrange("(a c) f -> c a f", c=P)
+            load(("w", g, h), src, "rows", 6)
+
+        def load_gate(i):
+            load(("gate", i), rows2(gate, i), "gate", 3)
+
+        x_rows = keep.tile([P, 4, PACK, K], BF16, name="x_rows")
+
+        def load_x(i):
+            src = x[i * G : (i + 1) * G, :].rearrange("(c e u) f -> c u e f", e=2, u=2)
+            for u in range(2):
+                nc.sync.dma_start(out=x_rows[:, i, 2 * u : 2 * u + 2, :], in_=src[:, u])
+
+        def new_bank(shape):
+            return psum.tile(shape, F32, name="bank", tag="bank", bufs=8)
+
+        def turn(key, rows, sorted_words):
+            pair = []
+            for b in range(2):
+                bank = new_bank([P, 2, 2, P])
+                for t in range(2):
+                    words = rows[2 * b + t].bitcast(F32)
+                    for u in range(2):
+                        part = words[:, u * P : (u + 1) * P] if sorted_words else words[:, u : 2 * P : 2]
+                        nc.tensor.transpose(bank[:, t, u, :], part, ident[:])
+                pair.append(bank)
+            banks[key] = pair
+
+        def new_packed(key):
+            packed[key] = work.tile([P, G * PACK], BF16, name="packed", tag="packed", bufs=7, align_bytes=64)
+            return packed[key]
+
+        def unturn(key):
+            words = new_packed(key)[:].bitcast(F32).rearrange("p (b t c u) -> p b t c u", b=2, t=2, u=2)
+            for b, bank in enumerate(banks[key]):
+                nc.scalar.copy(out=words[:, b], in_=bank[:].rearrange("p t u c -> p t c u"))
+
+        def quantise(key, fmt, tag, bufs):
+            codes = work.tile([P, G], U32, name=tag + "_codes", tag=tag + "_codes", bufs=bufs, align_bytes=64)
+            scales = work.tile([P, G], U8, name=tag + "_scales", tag=tag + "_scales", bufs=bufs, align_bytes=64)
+            nc.vector.quantize_mx(out=codes[:].bitcast(fmt), scales=scales[:], in_=packed[key][:])
+            mx[key] = (codes, scales, fmt)
+
+        def mx_pass(out, stationary, j, moving, start, stop):
+            cols = slice(j * P, (j + 1) * P)
+            nc.tensor.matmul_mx(
+                out=out[:],
+                lhsT=mx[stationary][0][:, cols].bitcast(mx[stationary][2]),
+                lhsT_scale=mx[stationary][1][:, cols],
+                rhs=mx[moving][0][:].bitcast(mx[moving][2]),
+                rhs_scale=mx[moving][1][:],
+                start=start,
+                stop=stop,
+            )
+
+        def turn_e(g):
+            turn(("e", g), [raw["e", g][:, t, :] for t in range(4)], False)
+            unturn(("e", g))
+
+        def turn_v(i):
+            turn(("v", i), [raw["v", i][:, a % 2, a // 2, :] for a in range(4)], False)
+            unturn(("v", i))
+
+        def turn_w(g, h):
+            turn(("w", g, h), [raw["w", g, h][:, a, :] for a in range(4)], False)
+            unturn(("w", g, h))
+
+        def turn_gate(s):
+            i, g = TILES[s]
+            key = ("gate", i, g)
+            turn(key, [raw["gate", i][:, a % 2, a // 2, g * G : (g + 1) * G] for a in range(4)], False)
+            tile = work.tile([P, 2, G, 2], BF16, name="gate_t", tag="gate_t", bufs=3)
+            words = tile[:].rearrange("p u j e -> p (u j e)").bitcast(F32).rearrange("p (u b t c) -> p b u t c", u=2, b=2, t=2)
+            for b, bank in enumerate(banks[key]):
+                nc.scalar.copy(out=words[:, b], in_=bank[:].rearrange("p t u c -> p u t c"))
+            packed[key] = tile
+
+        def turn_dh(s):
+            key = ("dh_m",) + TILES[s]
+            turn(key, [dh[s][:, t, :] for t in range(4)], True)
+            unturn(key)
+
+        def dz_pass(s, t):
+            i, g = TILES[s]
+            bank = new_bank([P, G])
+            mx_pass(bank, ("e", g), t, ("v", i), True, True)
+            dz[s, t] = bank
+
+        def make_dh(s, t):
+            i, g = TILES[s]
+            if t == 0:
+                dh[s] = work.tile([P, PACK, G], BF16, name="dh", tag="dh", bufs=3)
+            nc.vector.scalar_tensor_tensor(
+                out=dh[s][:, t, :],
+                in0=dz[s, t][:],
+                scalar=mean[:, g, t : t + 1],
+                in1=packed["gate", i, g][:, t // 2, :, t % 2],
+                op0=ADD,
+                op1=MULT,
+            )
+
+        def dx_group(i, h, a, copy):
+            bank = new_bank([P, G])
+            for g in range(2):
+                mx_pass(bank, ("dh_n", i, g), a, ("w", g, h), g == 0, g == 1)
+            res = work.tile([P, G], F32, name="res", tag="res", bufs=8)
+            copy(out=res[:], in_=bank[:])
+            nc.sync.dma_start(out=rows2(dx, i)[:, a % 2, a // 2, h * G : (h + 1) * G], in_=res[:])
+
+        def dw_group(g, j, copy):
+            bank = new_bank([P, G])
+            for i in range(4):
+                mx_pass(bank, ("x", j), i, ("dh_m", i, g), i == 0, i == 3)
+            res = work.tile([P, G], F32, name="res", tag="res", bufs=8)
+            copy(
+                out=res[:].rearrange("p (c t) -> p c t", t=PACK),
+                in_=bank[:].rearrange("p (t c) -> p c t", t=PACK),
+            )
+            nc.sync.dma_start(out=dw[j * P : (j + 1) * P, g * G : (g + 1) * G], in_=res[:])
+
+        def quant_e(g):
+            quantise(("e", g), E5M2, "e", 2)
+
+        def quant_v(i):
+            quantise(("v", i), E4M3, "v", 2)
+
+        def quant_w(g, h):
+            quantise(("w", g, h), E4M3, "w", 4)
+
+        def quant_x(j):
+            quantise(("x", j), E4M3, "x", 4)
+
+        def quant_dh_n(s):
+            quantise(("dh_n",) + TILES[s], E5M2, "dh_n", 4)
+
+        def quant_dh_m(s):
+            quantise(("dh_m",) + TILES[s], E5M2, "dh_m", 8)
+
+        def weave_x(j, copy):
+            copy(
+                out=new_packed(("x", j))[:].rearrange("p (b c i t) -> p b c t i", b=4, i=4, t=PACK),
+                in_=x_rows[:, :, :, j * P : (j + 1) * P].rearrange("p b t (c i) -> p b c t i", i=4),
+            )
+
+        def weave_dh(s, copy):
+            copy(
+                out=new_packed(("dh_n",) + TILES[s])[:].rearrange("p (c i t) -> p c t i", i=4, t=PACK),
+                in_=dh[s][:].rearrange("p t (c i) -> p c t i", i=4),
+            )
+
+        on_scalar = nc.scalar.copy
+        on_vector = nc.vector.tensor_copy
+
+        load_e(0)
+        load_v(0)
+        mean = keep.tile([P, 2, PACK], BF16, name="mean")
+        nc.sync.dma_start(out=mean[:], in_=mean_grad.rearrange("(g p t) -> p g t", g=2, t=PACK))
+        load_gate(0)
+        load_e(1)
+        load_w(0, 0)
+        load_v(1)
+        load_gate(1)
+        load_w(1, 0)
+
+        turn_e(0)
+        turn_v(0)
+        load_w(0, 1)
+        load_w(1, 1)
+        quant_e(0)
+        turn_gate(0)
+        quant_v(0)
+
+        E, V, W, D = (turn_e, quant_e), (turn_v, quant_v), (turn_w, quant_w), (turn_dh, quant_dh_m)
+        early = {0: (E, (1,)), 1: (V, (1,)), 2: (W, (0, 1)), 3: (V, (2,)), 5: (V, (3,)), 7: (D, (6,))}
+        late = {0: [(W, (0, 0))], 1: [(W, (1, 0))], 2: [(W, (1, 1))]}
+        loads = {
+            0: [(load_v, (2,)), (load_gate, (2,)), (load_x, (0,)), (load_x, (1,))],
+            1: [(load_v, (3,)), (load_x, (2,)), (load_x, (3,))],
+            2: [(load_gate, (3,))],
+        }
+        pending = []
+        for s, (i, g) in enumerate(TILES):
+            for t in range(4):
+                dz_pass(s, t)
+            for t in range(4):
+                make_dh(s, t)
+            if s in early:
+                early[s][0][0](*early[s][1])
+            if s + 1 < len(TILES):
+                turn_gate(s + 1)
+            for job, args in pending:
+                job[1](*args)
+            if s == 0:
+                quant_e(1)
+            if s in (5, 7):
+                quant_x((s - 5) // 2)
+            weave_dh(s, on_vector)
+            if s in early and s > 0:
+                early[s][0][1](*early[s][1])
+            quant_dh_n(s)
+            if i > 0:
+                for a in range(4):
+                    dx_group(i - 1, g, a, on_scalar)
+            pending = late.get(s, []) + ([(D, (s - 1 if s < 7 else s,))] if s > 0 else [])
+            for job, args in pending:
+                job[0](*args)
+            if s in (4, 6):
+                weave_x((s - 4) // 2, on_vector)
+            for fn, largs in loads.get(s, []):
+                fn(*largs)
+
+        quant_dh_m(7)
+        weave_x(2, on_vector)
+        for j in range(8):
+            dw_group(0, j, on_scalar)
+            dx_group(3, j // 4, j % 4, on_scalar)
+            dw_group(1, j, on_vector if j >= 6 else on_scalar)
+            if j + 2 < 8:
+                quant_x(j + 2)
+            if j + 3 < 8:
+                weave_x(j + 3, on_vector)

@@ -18,263 +18,283 @@ MULT = mybir.AluOpType.mult
 P = 128
 PACK = 4
 G = P * PACK
-TILES = [(i, g) for i in range(4) for g in range(2)]
+TILES = [(i, g) for i in range(M // G) for g in range(N // G)]
+LAST = len(TILES) - 1
+FIRST_SORTED = 3
+FIRST_DX = 3
+DX_PER_STEP = 4
 
 
 def tile_cross_moment_backward_s6_kernel(tc, v, e, mean_grad, gate, w, x, dx, dw):
     nc = tc.nc
+    on_scalar = nc.scalar.copy
+    on_vector = nc.vector.tensor_copy
     with ExitStack() as ctx:
         keep = ctx.enter_context(tc.tile_pool(name="keep", bufs=1))
         work = ctx.enter_context(tc.tile_pool(name="work", bufs=2))
-        psum = ctx.enter_context(tc.psum_pool(name="psum", bufs=2))
+        psum = ctx.enter_context(tc.psum_pool(name="psum", bufs=8))
         ctx.enter_context(tc.manual_schedule())
 
         ident = keep.tile([P, P], F32, name="ident")
         make_identity(nc, ident[:])
 
-        raw = {}
+        rows = {}
+        gate_t = {}
         packed = {}
         mx = {}
-        banks = {}
-        dz = {}
         dh = {}
 
-        def load(key, src, tag, bufs):
-            tile = work.tile(list(src.shape), BF16, name=tag, tag=tag, bufs=bufs)
-            nc.sync.dma_start(out=tile[:], in_=src)
-            raw[key] = tile
-
-        def rows4(src, i):
-            return src[i * G : (i + 1) * G, :].rearrange("(c t) f -> c t f", t=PACK)
-
-        def rows2(src, i):
+        def sample_rows(src, i):
             return src[i * G : (i + 1) * G, :].rearrange("(h c u) f -> c h u f", h=2, u=2)
 
-        def load_e(g):
-            load(("e", g), rows4(e, g), "rows", 6)
+        def load_rows(key, src):
+            tile = work.tile([P, 2, 2, G], BF16, name="rows", tag="rows", bufs=10)
+            nc.sync.dma_start(out=tile[:].rearrange("p a b f -> p (a b) f"), in_=src)
+            rows[key] = tile[:]
 
-        def load_v(i):
-            load(("v", i), rows2(v, i), "rows", 6)
+        def load_e(g):
+            load_rows(("e", g), e[g * G : (g + 1) * G, :].rearrange("(c t) f -> c t f", t=PACK))
 
         def load_w(g, h):
-            src = w[h * G : (h + 1) * G, g * G : (g + 1) * G].rearrange("(a c) f -> c a f", c=P)
-            load(("w", g, h), src, "rows", 6)
+            load_rows(("w", g, h), w[h * G : (h + 1) * G, g * G : (g + 1) * G].rearrange("(a c) f -> c a f", c=P))
 
-        def load_gate(i):
-            load(("gate", i), rows2(gate, i), "gate", 3)
+        def load_v(i):
+            tile = work.tile([P, 2, 2, G], BF16, name="rows", tag="rows", bufs=10)
+            nc.sync.dma_start(out=tile[:], in_=sample_rows(v, i))
+            rows["v", i] = tile[:].rearrange("p h u f -> p u h f")
 
-        x_rows = keep.tile([P, 4, PACK, K], BF16, name="x_rows")
+        def load_gate(s):
+            i, g = TILES[s]
+            tile = work.tile([P, 2, 2, G], BF16, name="gate", tag="gate", bufs=5)
+            for h in range(2):
+                nc.sync.dma_start(out=tile[:, h], in_=sample_rows(gate, i)[:, h, :, g * G : (g + 1) * G])
+            rows["gate", s] = tile[:].rearrange("p h u f -> p u h f")
+
+        x_rows = keep.tile([P, M // G, PACK, K], BF16, name="x_rows")
 
         def load_x(i):
-            src = x[i * G : (i + 1) * G, :].rearrange("(c e u) f -> c u e f", e=2, u=2)
+            src = x[i * G : (i + 1) * G, :].rearrange("(c f u) k -> c u f k", f=2, u=2)
             for u in range(2):
                 nc.sync.dma_start(out=x_rows[:, i, 2 * u : 2 * u + 2, :], in_=src[:, u])
 
         def new_bank(shape):
-            return psum.tile(shape, F32, name="bank", tag="bank", bufs=8)
+            return psum.tile(shape, F32, name="bank", tag="bank")
 
-        def turn(key, rows, sorted_words):
-            pair = []
-            for b in range(2):
+        def new_packed(key, tag="packed", bufs=6):
+            packed[key] = work.tile([P, G * PACK], BF16, name=tag, tag=tag, bufs=bufs, align_bytes=64)
+            return packed[key][:]
+
+        def new_woven(key):
+            return new_packed(key, "woven", 1)
+
+        def transposes(src, contiguous):
+            banks = []
+            for a in range(2):
                 bank = new_bank([P, 2, 2, P])
-                for t in range(2):
-                    words = rows[2 * b + t].bitcast(F32)
+                for b in range(2):
+                    words = src[:, a, b, :].bitcast(F32)
                     for u in range(2):
-                        part = words[:, u * P : (u + 1) * P] if sorted_words else words[:, u : 2 * P : 2]
-                        nc.tensor.transpose(bank[:, t, u, :], part, ident[:])
-                pair.append(bank)
-            banks[key] = pair
+                        part = words[:, u * P : (u + 1) * P] if contiguous else words[:, u : 2 * P : 2]
+                        nc.tensor.transpose(bank[:, b, u, :], part, ident[:])
+                banks.append(bank)
+            return banks
 
-        def new_packed(key):
-            packed[key] = work.tile([P, G * PACK], BF16, name="packed", tag="packed", bufs=7, align_bytes=64)
-            return packed[key]
+        def pack_banks(banks, dst, copies):
+            words = dst.bitcast(F32).rearrange("p (a b c u) -> p a b c u", a=2, b=2, u=2)
+            for a in range(2):
+                copies[a](out=words[:, a], in_=banks[a][:].rearrange("p b u c -> p b c u"))
 
-        def unturn(key):
-            words = new_packed(key)[:].bitcast(F32).rearrange("p (b t c u) -> p b t c u", b=2, t=2, u=2)
-            for b, bank in enumerate(banks[key]):
-                nc.scalar.copy(out=words[:, b], in_=bank[:].rearrange("p t u c -> p t c u"))
+        def turn(key, copies=(on_scalar, on_scalar), alloc=new_packed):
+            pack_banks(transposes(rows[key], False), alloc(key), copies)
 
-        def quantise(key, fmt, tag, bufs):
-            codes = work.tile([P, G], U32, name=tag + "_codes", tag=tag + "_codes", bufs=bufs, align_bytes=64)
-            scales = work.tile([P, G], U8, name=tag + "_scales", tag=tag + "_scales", bufs=bufs, align_bytes=64)
-            nc.vector.quantize_mx(out=codes[:].bitcast(fmt), scales=scales[:], in_=packed[key][:])
+        def turn_dh(s):
+            src = dh[s][:].rearrange("p (a b) j -> p a b j", a=2)
+            pack_banks(transposes(src, True), new_packed(("dh_m", s)), (on_scalar, on_scalar))
+
+        def sort_gate(s):
+            tile = work.tile([P, 2, 2, G], BF16, name="sorted", tag="sorted", bufs=3)
+            on_vector(
+                out=tile[:].bitcast(F32).rearrange("p a b (u c) -> p a b u c", u=2),
+                in_=rows["gate", s].bitcast(F32).rearrange("p a b (c u) -> p a b u c", u=2),
+            )
+            rows["gate", s] = tile[:]
+
+        def turn_gate(s):
+            banks = transposes(rows["gate", s], s >= FIRST_SORTED)
+            tile = work.tile([P, 2, G, 2], BF16, name="gate_t", tag="gate_t", bufs=3)
+            words = tile[:].rearrange("p u j f -> p (u j f)").bitcast(F32)
+            words = words.rearrange("p (u a b c) -> p a u b c", u=2, a=2, b=2)
+            for a in range(2):
+                on_scalar(out=words[:, a], in_=banks[a][:].rearrange("p b u c -> p u b c"))
+            gate_t[s] = tile
+
+        def weave_on_vector(dst, src):
+            on_vector(
+                out=dst.rearrange("p (b c r t) -> p b c t r", b=src.shape[1], r=4, t=PACK),
+                in_=src.rearrange("p b t (c r) -> p b c t r", r=4),
+            )
+
+        def weave_x(j):
+            weave_on_vector(new_packed(("x", j)), x_rows[:, :, :, j * P : (j + 1) * P])
+
+        def weave_dh_on_gpsimd(s):
+            nc.gpsimd.tensor_scalar(
+                out=new_woven(("dh_n", s)).rearrange("p (j t) -> p j t", t=PACK),
+                in0=dh[s][:].rearrange("p t j -> p j t"),
+                scalar1=1.0,
+                scalar2=0.0,
+                op0=MULT,
+                op1=ADD,
+            )
+
+        kinds = {"v": (E4M3, 2), "e": (E5M2, 2), "w": (E4M3, 4), "x": (E4M3, 4), "dh_n": (E5M2, 4), "dh_m": (E5M2, 8)}
+
+        def quantise(key, parts=1):
+            fmt, bufs = kinds[key[0]]
+            codes = work.tile([P, G], U32, name="codes", tag=key[0] + "_codes", bufs=bufs, align_bytes=64)
+            scales = work.tile([P, G], U8, name="scales", tag=key[0] + "_scales", bufs=bufs, align_bytes=64)
+            for n in range(parts):
+                lo, hi = n * G // parts, (n + 1) * G // parts
+                nc.vector.quantize_mx(
+                    out=codes[:, lo:hi].bitcast(fmt), scales=scales[:, lo:hi], in_=packed[key][:, lo * PACK : hi * PACK]
+                )
             mx[key] = (codes, scales, fmt)
 
-        def mx_pass(out, stationary, j, moving, start, stop):
-            cols = slice(j * P, (j + 1) * P)
+        def mx_pass(bank, stationary, a, moving, start, stop):
+            codes, scales, fmt = mx[stationary]
+            cols = slice(a * P, (a + 1) * P)
             nc.tensor.matmul_mx(
-                out=out[:],
-                lhsT=mx[stationary][0][:, cols].bitcast(mx[stationary][2]),
-                lhsT_scale=mx[stationary][1][:, cols],
+                out=bank[:],
+                lhsT=codes[:, cols].bitcast(fmt),
+                lhsT_scale=scales[:, cols],
                 rhs=mx[moving][0][:].bitcast(mx[moving][2]),
                 rhs_scale=mx[moving][1][:],
                 start=start,
                 stop=stop,
             )
 
-        def turn_e(g):
-            turn(("e", g), [raw["e", g][:, t, :] for t in range(4)], False)
-            unturn(("e", g))
-
-        def turn_v(i):
-            turn(("v", i), [raw["v", i][:, a % 2, a // 2, :] for a in range(4)], False)
-            unturn(("v", i))
-
-        def turn_w(g, h):
-            turn(("w", g, h), [raw["w", g, h][:, a, :] for a in range(4)], False)
-            unturn(("w", g, h))
-
-        def turn_gate(s):
+        def make_dh(s):
             i, g = TILES[s]
-            key = ("gate", i, g)
-            turn(key, [raw["gate", i][:, a % 2, a // 2, g * G : (g + 1) * G] for a in range(4)], False)
-            tile = work.tile([P, 2, G, 2], BF16, name="gate_t", tag="gate_t", bufs=3)
-            words = tile[:].rearrange("p u j e -> p (u j e)").bitcast(F32).rearrange("p (u b t c) -> p b u t c", u=2, b=2, t=2)
-            for b, bank in enumerate(banks[key]):
-                nc.scalar.copy(out=words[:, b], in_=bank[:].rearrange("p t u c -> p u t c"))
-            packed[key] = tile
+            dz = []
+            for t in range(PACK):
+                bank = new_bank([P, G])
+                mx_pass(bank, ("e", g), t, ("v", i), True, True)
+                dz.append(bank)
+            dh[s] = work.tile([P, PACK, G], BF16, name="dh", tag="dh", bufs=3)
+            for t in range(PACK):
+                nc.vector.scalar_tensor_tensor(
+                    out=dh[s][:, t, :],
+                    in0=dz[t][:],
+                    scalar=mean[:, g, t : t + 1],
+                    in1=gate_t[s][:, t // 2, :, t % 2],
+                    op0=ADD,
+                    op1=MULT,
+                )
 
-        def turn_dh(s):
-            key = ("dh_m",) + TILES[s]
-            turn(key, [dh[s][:, t, :] for t in range(4)], True)
-            unturn(key)
+        def new_result():
+            return work.tile([P, G], F32, name="result", tag="result", bufs=8)
 
-        def dz_pass(s, t):
-            i, g = TILES[s]
-            bank = new_bank([P, G])
-            mx_pass(bank, ("e", g), t, ("v", i), True, True)
-            dz[s, t] = bank
-
-        def make_dh(s, t):
-            i, g = TILES[s]
-            if t == 0:
-                dh[s] = work.tile([P, PACK, G], BF16, name="dh", tag="dh", bufs=3)
-            nc.vector.scalar_tensor_tensor(
-                out=dh[s][:, t, :],
-                in0=dz[s, t][:],
-                scalar=mean[:, g, t : t + 1],
-                in1=packed["gate", i, g][:, t // 2, :, t % 2],
-                op0=ADD,
-                op1=MULT,
-            )
-
-        def dx_group(i, h, a, copy):
+        def dx_bank(i, h, a, copy=on_scalar):
             bank = new_bank([P, G])
             for g in range(2):
-                mx_pass(bank, ("dh_n", i, g), a, ("w", g, h), g == 0, g == 1)
-            res = work.tile([P, G], F32, name="res", tag="res", bufs=8)
+                mx_pass(bank, ("dh_n", 2 * i + g), a, ("w", g, h), g == 0, g == 1)
+            res = new_result()
             copy(out=res[:], in_=bank[:])
-            nc.sync.dma_start(out=rows2(dx, i)[:, a % 2, a // 2, h * G : (h + 1) * G], in_=res[:])
+            nc.sync.dma_start(out=sample_rows(dx, i)[:, a % 2, a // 2, h * G : (h + 1) * G], in_=res[:])
 
-        def dw_group(g, j, copy):
+        def dw_bank(g, j, copy=on_scalar):
             bank = new_bank([P, G])
-            for i in range(4):
-                mx_pass(bank, ("x", j), i, ("dh_m", i, g), i == 0, i == 3)
-            res = work.tile([P, G], F32, name="res", tag="res", bufs=8)
-            copy(
-                out=res[:].rearrange("p (c t) -> p c t", t=PACK),
-                in_=bank[:].rearrange("p (t c) -> p c t", t=PACK),
-            )
+            for i in range(M // G):
+                mx_pass(bank, ("x", j), i, ("dh_m", 2 * i + g), i == 0, i == M // G - 1)
+            res = new_result()
+            copy(out=res[:].rearrange("p (c t) -> p c t", t=PACK), in_=bank[:].rearrange("p (t c) -> p c t", t=PACK))
             nc.sync.dma_start(out=dw[j * P : (j + 1) * P, g * G : (g + 1) * G], in_=res[:])
 
-        def quant_e(g):
-            quantise(("e", g), E5M2, "e", 2)
-
-        def quant_v(i):
-            quantise(("v", i), E4M3, "v", 2)
-
-        def quant_w(g, h):
-            quantise(("w", g, h), E4M3, "w", 4)
-
-        def quant_x(j):
-            quantise(("x", j), E4M3, "x", 4)
-
-        def quant_dh_n(s):
-            quantise(("dh_n",) + TILES[s], E5M2, "dh_n", 4)
-
-        def quant_dh_m(s):
-            quantise(("dh_m",) + TILES[s], E5M2, "dh_m", 8)
-
-        def weave_x(j, copy):
-            copy(
-                out=new_packed(("x", j))[:].rearrange("p (b c i t) -> p b c t i", b=4, i=4, t=PACK),
-                in_=x_rows[:, :, :, j * P : (j + 1) * P].rearrange("p b t (c i) -> p b c t i", i=4),
-            )
-
-        def weave_dh(s, copy):
-            copy(
-                out=new_packed(("dh_n",) + TILES[s])[:].rearrange("p (c i t) -> p c t i", i=4, t=PACK),
-                in_=dh[s][:].rearrange("p t (c i) -> p c t i", i=4),
-            )
-
-        on_scalar = nc.scalar.copy
-        on_vector = nc.vector.tensor_copy
-
-        load_e(0)
         load_v(0)
+        load_gate(0)
+        load_e(0)
         mean = keep.tile([P, 2, PACK], BF16, name="mean")
         nc.sync.dma_start(out=mean[:], in_=mean_grad.rearrange("(g p t) -> p g t", g=2, t=PACK))
-        load_gate(0)
         load_e(1)
-        load_w(0, 0)
-        load_v(1)
         load_gate(1)
+        load_v(1)
+        load_w(0, 0)
+        load_gate(2)
         load_w(1, 0)
 
-        turn_e(0)
-        turn_v(0)
-        load_w(0, 1)
-        load_w(1, 1)
-        quant_e(0)
+        turn(("v", 0), (on_scalar, on_vector))
+        quantise(("v", 0))
         turn_gate(0)
-        quant_v(0)
+        load_w(0, 1)
+        load_gate(3)
+        load_w(1, 1)
+        turn(("e", 0), (on_vector, on_scalar))
+        turn(("e", 1))
+        quantise(("e", 0), parts=2)
 
-        E, V, W, D = (turn_e, quant_e), (turn_v, quant_v), (turn_w, quant_w), (turn_dh, quant_dh_m)
-        early = {0: (E, (1,)), 1: (V, (1,)), 2: (W, (0, 1)), 3: (V, (2,)), 5: (V, (3,)), 7: (D, (6,))}
-        late = {0: [(W, (0, 0))], 1: [(W, (1, 0))], 2: [(W, (1, 1))]}
+        early = {0: ("v", 1), 1: ("w", 0, 0), 2: ("w", 0, 1), 3: ("v", 2), 5: ("v", 3)}
+        late = {1: ("w", 1, 0), 2: ("w", 1, 1)}
         loads = {
-            0: [(load_v, (2,)), (load_gate, (2,)), (load_x, (0,)), (load_x, (1,))],
-            1: [(load_v, (3,)), (load_x, (2,)), (load_x, (3,))],
-            2: [(load_gate, (3,))],
+            0: [(load_v, 2), (load_gate, 4), (load_gate, 5)],
+            1: [(load_v, 3), (load_gate, 6), (load_x, 0), (load_x, 1)],
+            2: [(load_gate, 7), (load_x, 2), (load_x, 3)],
         }
-        pending = []
-        for s, (i, g) in enumerate(TILES):
-            for t in range(4):
-                dz_pass(s, t)
-            for t in range(4):
-                make_dh(s, t)
-            if s in early:
-                early[s][0][0](*early[s][1])
-            if s + 1 < len(TILES):
-                turn_gate(s + 1)
-            for job, args in pending:
-                job[1](*args)
-            if s == 0:
-                quant_e(1)
-            if s in (5, 7):
-                quant_x((s - 5) // 2)
-            weave_dh(s, on_vector)
-            if s in early and s > 0:
-                early[s][0][1](*early[s][1])
-            quant_dh_n(s)
-            if i > 0:
-                for a in range(4):
-                    dx_group(i - 1, g, a, on_scalar)
-            pending = late.get(s, []) + ([(D, (s - 1 if s < 7 else s,))] if s > 0 else [])
-            for job, args in pending:
-                job[0](*args)
-            if s in (4, 6):
-                weave_x((s - 4) // 2, on_vector)
-            for fn, largs in loads.get(s, []):
-                fn(*largs)
+        dx_banks = [(i, h, a) for i in range(M // G) for h in range(2) for a in range(4)]
 
-        quant_dh_m(7)
-        weave_x(2, on_vector)
-        for j in range(8):
-            dw_group(0, j, on_scalar)
-            dx_group(3, j // 4, j % 4, on_scalar)
-            dw_group(1, j, on_vector if j >= 6 else on_scalar)
-            if j + 2 < 8:
-                quant_x(j + 2)
-            if j + 3 < 8:
-                weave_x(j + 3, on_vector)
+        unquantised = [("e", 1)]
+        for s in range(len(TILES)):
+            todo = dx_banks[DX_PER_STEP * (s - FIRST_DX) :][:DX_PER_STEP] if s >= FIRST_DX else []
+            make_dh(s)
+            for n, args in enumerate(todo[:2]):
+                dx_bank(*args, on_scalar if n else on_vector)
+            if s in early:
+                turn(early[s], alloc=new_packed if s else new_woven)
+            if s < LAST:
+                turn_gate(s + 1)
+            for key in unquantised:
+                quantise(key)
+            unquantised = []
+            if s > 0:
+                turn_dh(s - 1)
+                unquantised.append(("dh_m", s - 1))
+            if s in early:
+                quantise(early[s])
+            if FIRST_SORTED <= s + 2 <= LAST:
+                sort_gate(s + 2)
+            if s > 0:
+                quantise(("dh_n", s - 1))
+            if s < LAST:
+                weave_dh_on_gpsimd(s)
+            else:
+                weave_on_vector(new_packed(("dh_n", s)), dh[s][:].rearrange("p (b t) j -> p b t j", b=1))
+            for args in todo[2:]:
+                dx_bank(*args)
+            if s in late:
+                turn(late[s])
+                unquantised = [late[s]] + unquantised
+            for load, index in loads.get(s, []):
+                load(index)
+
+        rest = dx_banks[DX_PER_STEP * (len(TILES) - FIRST_DX) :]
+        for args in rest[:4]:
+            dx_bank(*args)
+        turn_dh(LAST)
+        quantise(("dh_m", LAST - 1))
+        quantise(("dh_n", LAST))
+        weave_x(0)
+        for args in rest[4:10]:
+            dx_bank(*args)
+        quantise(("dh_m", LAST))
+        quantise(("x", 0))
+        weave_x(1)
+
+        slices = K // P
+        for j in range(slices):
+            dw_bank(0, j)
+            if j + 1 < slices:
+                quantise(("x", j + 1))
+            if j + 2 < slices:
+                weave_x(j + 2)
+            dw_bank(1, j, on_scalar if j + 2 < slices else on_vector)
+            for args in rest[10 + j : 11 + j]:
+                dx_bank(*args)

@@ -20,8 +20,9 @@ PACK = 4
 G = P * PACK
 TILES = [(i, g) for i in range(M // G) for g in range(N // G)]
 LAST = len(TILES) - 1
-FIRST_SORTED = 3
+FIRST_SORTED = 2
 FIRST_DX = 3
+GPSIMD_COLS = 384
 DX_PER_STEP = 4
 
 
@@ -139,12 +140,18 @@ def tile_cross_moment_backward_s6_kernel(tc, v, e, mean_grad, gate, w, x, dx, dw
 
         def weave_dh_on_gpsimd(s):
             nc.gpsimd.tensor_scalar(
-                out=new_woven(("dh_n", s)).rearrange("p (j t) -> p j t", t=PACK),
-                in0=dh[s][:].rearrange("p t j -> p j t"),
+                out=new_woven(("dh_n", s))[:, : GPSIMD_COLS * PACK].rearrange("p (j t) -> p j t", t=PACK),
+                in0=dh[s][:, :, :GPSIMD_COLS].rearrange("p t j -> p j t"),
                 scalar1=1.0,
                 scalar2=0.0,
                 op0=MULT,
                 op1=ADD,
+            )
+
+        def weave_dh_on_scalar(s):
+            on_scalar(
+                out=packed["dh_n", s][:, GPSIMD_COLS * PACK :].rearrange("p (c r t) -> p c t r", r=4, t=PACK),
+                in_=dh[s][:, :, GPSIMD_COLS:].rearrange("p t (c r) -> p c t r", r=4),
             )
 
         kinds = {"v": (E4M3, 2), "e": (E5M2, 2), "w": (E4M3, 4), "x": (E4M3, 4), "dh_n": (E5M2, 4), "dh_m": (E5M2, 8)}
@@ -272,6 +279,8 @@ def tile_cross_moment_backward_s6_kernel(tc, v, e, mean_grad, gate, w, x, dx, dw
             if s in late:
                 turn(late[s])
                 unquantised = [late[s]] + unquantised
+            if s < LAST:
+                weave_dh_on_scalar(s)
             for load, index in loads.get(s, []):
                 load(index)
 

@@ -22,7 +22,7 @@ TILES = [(i, g) for i in range(M // G) for g in range(N // G)]
 LAST = len(TILES) - 1
 FIRST_SORTED = 2
 FIRST_DX = 3
-GPSIMD_COLS = 384
+GPSIMD_COLS = 448
 DX_PER_STEP = 4
 
 
@@ -199,7 +199,7 @@ def tile_cross_moment_backward_s6_kernel(tc, v, e, mean_grad, gate, w, x, dx, dw
                 )
 
         def new_result():
-            return work.tile([P, G], F32, name="result", tag="result", bufs=8)
+            return work.tile([P, G], F32, name="result", tag="result", bufs=10)
 
         def dx_bank(i, h, a, copy=on_scalar):
             bank = new_bank([P, G])
@@ -243,8 +243,11 @@ def tile_cross_moment_backward_s6_kernel(tc, v, e, mean_grad, gate, w, x, dx, dw
         late = {1: ("w", 1, 0), 2: ("w", 1, 1)}
         loads = {
             0: [(load_v, 2), (load_gate, 4), (load_gate, 5)],
-            1: [(load_v, 3), (load_gate, 6), (load_x, 0), (load_x, 1)],
-            2: [(load_gate, 7), (load_x, 2), (load_x, 3)],
+            1: [(load_v, 3), (load_gate, 6)],
+            2: [(load_gate, 7), (load_x, 0)],
+            3: [(load_x, 1)],
+            4: [(load_x, 2)],
+            5: [(load_x, 3)],
         }
         dx_banks = [(i, h, a) for i in range(M // G) for h in range(2) for a in range(4)]
 
@@ -285,13 +288,13 @@ def tile_cross_moment_backward_s6_kernel(tc, v, e, mean_grad, gate, w, x, dx, dw
                 load(index)
 
         rest = dx_banks[DX_PER_STEP * (len(TILES) - FIRST_DX) :]
-        for args in rest[:4]:
+        for args in rest[:DX_PER_STEP]:
             dx_bank(*args)
         turn_dh(LAST)
         quantise(("dh_m", LAST - 1))
         quantise(("dh_n", LAST))
         weave_x(0)
-        for args in rest[4:10]:
+        for args in rest[DX_PER_STEP:]:
             dx_bank(*args)
         quantise(("dh_m", LAST))
         quantise(("x", 0))
@@ -305,5 +308,3 @@ def tile_cross_moment_backward_s6_kernel(tc, v, e, mean_grad, gate, w, x, dx, dw
             if j + 2 < slices:
                 weave_x(j + 2)
             dw_bank(1, j, on_scalar if j + 2 < slices else on_vector)
-            for args in rest[10 + j : 11 + j]:
-                dx_bank(*args)

from contextlib import ExitStack

import concourse.mybir as mybir
from concourse.masks import make_identity

M, Q, N, K = 2048, 512, 1024, 1024
FLOPS = 2 * M * N * Q + 2 * M * K * N + 2 * K * N * M

F32 = mybir.dt.float32
BF16 = mybir.dt.bfloat16
U32 = mybir.dt.uint32
U8 = mybir.dt.uint8
E4M3 = mybir.dt.float8_e4m3fn_x4
E5M2 = mybir.dt.float8_e5m2_x4
ADD = mybir.AluOpType.add
MULT = mybir.AluOpType.mult

P = 128
PACK = 4
G = P * PACK
TILES = [(i, g) for i in range(M // G) for g in range(N // G)]
LAST = len(TILES) - 1
FIRST_SORTED = 2
FIRST_DX = 3
GPSIMD_COLS = 448
DX_PER_STEP = 4


def tile_cross_moment_backward_s6_kernel(tc, v, e, mean_grad, gate, w, x, dx, dw):
    nc = tc.nc
    on_scalar = nc.scalar.copy
    on_vector = nc.vector.tensor_copy
    with ExitStack() as ctx:
        keep = ctx.enter_context(tc.tile_pool(name="keep", bufs=1))
        work = ctx.enter_context(tc.tile_pool(name="work", bufs=2))
        psum = ctx.enter_context(tc.psum_pool(name="psum", bufs=8))
        ctx.enter_context(tc.manual_schedule())

        ident = keep.tile([P, P], F32, name="ident")
        make_identity(nc, ident[:])

        rows = {}
        gate_t = {}
        packed = {}
        mx = {}
        dh = {}

        def sample_rows(src, i):
            return src[i * G : (i + 1) * G, :].rearrange("(h c u) f -> c h u f", h=2, u=2)

        def load_rows(key, src):
            tile = work.tile([P, 2, 2, G], BF16, name="rows", tag="rows", bufs=10)
            nc.sync.dma_start(out=tile[:].rearrange("p a b f -> p (a b) f"), in_=src)
            rows[key] = tile[:]

        def load_e(g):
            load_rows(("e", g), e[g * G : (g + 1) * G, :].rearrange("(c t) f -> c t f", t=PACK))

        def load_w(g, h):
            load_rows(("w", g, h), w[h * G : (h + 1) * G, g * G : (g + 1) * G].rearrange("(a c) f -> c a f", c=P))

        def load_v(i):
            tile = work.tile([P, 2, 2, G], BF16, name="rows", tag="rows", bufs=10)
            nc.sync.dma_start(out=tile[:], in_=sample_rows(v, i))
            rows["v", i] = tile[:].rearrange("p h u f -> p u h f")

        def load_gate(s):
            i, g = TILES[s]
            tile = work.tile([P, 2, 2, G], BF16, name="gate", tag="gate", bufs=5)
            for h in range(2):
                nc.sync.dma_start(out=tile[:, h], in_=sample_rows(gate, i)[:, h, :, g * G : (g + 1) * G])
            rows["gate", s] = tile[:].rearrange("p h u f -> p u h f")

        x_rows = keep.tile([P, M // G, PACK, K], BF16, name="x_rows")

        def load_x(i):
            src = x[i * G : (i + 1) * G, :].rearrange("(c f u) k -> c u f k", f=2, u=2)
            for u in range(2):
                nc.sync.dma_start(out=x_rows[:, i, 2 * u : 2 * u + 2, :], in_=src[:, u])

        def new_bank(shape):
            return psum.tile(shape, F32, name="bank", tag="bank")

        def new_packed(key, tag="packed", bufs=6):
            packed[key] = work.tile([P, G * PACK], BF16, name=tag, tag=tag, bufs=bufs, align_bytes=64)
            return packed[key][:]

        def new_woven(key):
            return new_packed(key, "woven", 1)

        def transposes(src, contiguous):
            banks = []
            for a in range(2):
                bank = new_bank([P, 2, 2, P])
                for b in range(2):
                    words = src[:, a, b, :].bitcast(F32)
                    for u in range(2):
                        part = words[:, u * P : (u + 1) * P] if contiguous else words[:, u : 2 * P : 2]
                        nc.tensor.transpose(bank[:, b, u, :], part, ident[:])
                banks.append(bank)
            return banks

        def pack_banks(banks, dst, copies):
            words = dst.bitcast(F32).rearrange("p (a b c u) -> p a b c u", a=2, b=2, u=2)
            for a in range(2):
                copies[a](out=words[:, a], in_=banks[a][:].rearrange("p b u c -> p b c u"))

        def turn(key, copies=(on_scalar, on_scalar), alloc=new_packed):
            pack_banks(transposes(rows[key], False), alloc(key), copies)

        def turn_dh(s):
            src = dh[s][:].rearrange("p (a b) j -> p a b j", a=2)
            pack_banks(transposes(src, True), new_packed(("dh_m", s)), (on_scalar, on_scalar))

        def sort_gate(s):
            tile = work.tile([P, 2, 2, G], BF16, name="sorted", tag="sorted", bufs=3)
            on_vector(
                out=tile[:].bitcast(F32).rearrange("p a b (u c) -> p a b u c", u=2),
                in_=rows["gate", s].bitcast(F32).rearrange("p a b (c u) -> p a b u c", u=2),
            )
            rows["gate", s] = tile[:]

        def turn_gate(s):
            banks = transposes(rows["gate", s], s >= FIRST_SORTED)
            tile = work.tile([P, 2, G, 2], BF16, name="gate_t", tag="gate_t", bufs=3)
            words = tile[:].rearrange("p u j f -> p (u j f)").bitcast(F32)
            words = words.rearrange("p (u a b c) -> p a u b c", u=2, a=2, b=2)
            for a in range(2):
                on_scalar(out=words[:, a], in_=banks[a][:].rearrange("p b u c -> p u b c"))
            gate_t[s] = tile

        def weave_on_vector(dst, src):
            on_vector(
                out=dst.rearrange("p (b c r t) -> p b c t r", b=src.shape[1], r=4, t=PACK),
                in_=src.rearrange("p b t (c r) -> p b c t r", r=4),
            )

        def weave_x(j):
            weave_on_vector(new_packed(("x", j)), x_rows[:, :, :, j * P : (j + 1) * P])

        def weave_dh_on_gpsimd(s):
            nc.gpsimd.tensor_scalar(
                out=new_woven(("dh_n", s))[:, : GPSIMD_COLS * PACK].rearrange("p (j t) -> p j t", t=PACK),
                in0=dh[s][:, :, :GPSIMD_COLS].rearrange("p t j -> p j t"),
                scalar1=1.0,
                scalar2=0.0,
                op0=MULT,
                op1=ADD,
            )

        def weave_dh_on_scalar(s):
            on_scalar(
                out=packed["dh_n", s][:, GPSIMD_COLS * PACK :].rearrange("p (c r t) -> p c t r", r=4, t=PACK),
                in_=dh[s][:, :, GPSIMD_COLS:].rearrange("p t (c r) -> p c t r", r=4),
            )

        kinds = {"v": (E4M3, 2), "e": (E5M2, 2), "w": (E4M3, 4), "x": (E4M3, 4), "dh_n": (E5M2, 4), "dh_m": (E5M2, 8)}

        def quantise(key, parts=1):
            fmt, bufs = kinds[key[0]]
            codes = work.tile([P, G], U32, name="codes", tag=key[0] + "_codes", bufs=bufs, align_bytes=64)
            scales = work.tile([P, G], U8, name="scales", tag=key[0] + "_scales", bufs=bufs, align_bytes=64)
            for n in range(parts):
                lo, hi = n * G // parts, (n + 1) * G // parts
                nc.vector.quantize_mx(
                    out=codes[:, lo:hi].bitcast(fmt), scales=scales[:, lo:hi], in_=packed[key][:, lo * PACK : hi * PACK]
                )
            mx[key] = (codes, scales, fmt)

        def mx_pass(bank, stationary, a, moving, start, stop):
            codes, scales, fmt = mx[stationary]
            cols = slice(a * P, (a + 1) * P)
            nc.tensor.matmul_mx(
                out=bank[:],
                lhsT=codes[:, cols].bitcast(fmt),
                lhsT_scale=scales[:, cols],
                rhs=mx[moving][0][:].bitcast(mx[moving][2]),
                rhs_scale=mx[moving][1][:],
                start=start,
                stop=stop,
            )

        def make_dh(s):
            i, g = TILES[s]
            dz = []
            for t in range(PACK):
                bank = new_bank([P, G])
                mx_pass(bank, ("e", g), t, ("v", i), True, True)
                dz.append(bank)
            dh[s] = work.tile([P, PACK, G], BF16, name="dh", tag="dh", bufs=3)
            for t in range(PACK):
                nc.vector.scalar_tensor_tensor(
                    out=dh[s][:, t, :],
                    in0=dz[t][:],
                    scalar=mean[:, g, t : t + 1],
                    in1=gate_t[s][:, t // 2, :, t % 2],
                    op0=ADD,
                    op1=MULT,
                )

        def new_result():
            return work.tile([P, G], F32, name="result", tag="result", bufs=10)

        def dx_bank(i, h, a, copy=on_scalar):
            bank = new_bank([P, G])
            for g in range(2):
                mx_pass(bank, ("dh_n", 2 * i + g), a, ("w", g, h), g == 0, g == 1)
            res = new_result()
            copy(out=res[:], in_=bank[:])
            nc.sync.dma_start(out=sample_rows(dx, i)[:, a % 2, a // 2, h * G : (h + 1) * G], in_=res[:])

        def dw_bank(g, j, copy=on_scalar):
            bank = new_bank([P, G])
            for i in range(M // G):
                mx_pass(bank, ("x", j), i, ("dh_m", 2 * i + g), i == 0, i == M // G - 1)
            res = new_result()
            copy(out=res[:].rearrange("p (c t) -> p c t", t=PACK), in_=bank[:].rearrange("p (t c) -> p c t", t=PACK))
            nc.sync.dma_start(out=dw[j * P : (j + 1) * P, g * G : (g + 1) * G], in_=res[:])

        load_v(0)
        load_gate(0)
        load_e(0)
        mean = keep.tile([P, 2, PACK], BF16, name="mean")
        nc.sync.dma_start(out=mean[:], in_=mean_grad.rearrange("(g p t) -> p g t", g=2, t=PACK))
        load_e(1)
        load_gate(1)
        load_v(1)
        load_w(0, 0)
        load_gate(2)
        load_w(1, 0)

        turn(("v", 0), (on_scalar, on_vector))
        quantise(("v", 0))
        turn_gate(0)
        load_w(0, 1)
        load_gate(3)
        load_w(1, 1)
        turn(("e", 0), (on_vector, on_scalar))
        turn(("e", 1))
        quantise(("e", 0), parts=2)

        early = {0: ("v", 1), 1: ("w", 0, 0), 2: ("w", 0, 1), 3: ("v", 2), 5: ("v", 3)}
        late = {1: ("w", 1, 0), 2: ("w", 1, 1)}
        loads = {
            0: [(load_v, 2), (load_gate, 4), (load_gate, 5)],
            1: [(load_v, 3), (load_gate, 6)],
            2: [(load_gate, 7), (load_x, 0)],
            3: [(load_x, 1)],
            4: [(load_x, 2)],
            5: [(load_x, 3)],
        }
        dx_banks = [(i, h, a) for i in range(M // G) for h in range(2) for a in range(4)]

        unquantised = [("e", 1)]
        for s in range(len(TILES)):
            todo = dx_banks[DX_PER_STEP * (s - FIRST_DX) :][:DX_PER_STEP] if s >= FIRST_DX else []
            make_dh(s)
            for n, args in enumerate(todo[:2]):
                dx_bank(*args, on_scalar if n else on_vector)
            if s in early:
                turn(early[s], alloc=new_packed if s else new_woven)
            if s < LAST:
                turn_gate(s + 1)
            for key in unquantised:
                quantise(key)
            unquantised = []
            if s > 0:
                turn_dh(s - 1)
                unquantised.append(("dh_m", s - 1))
            if s in early:
                quantise(early[s])
            if FIRST_SORTED <= s + 2 <= LAST:
                sort_gate(s + 2)
            if s > 0:
                quantise(("dh_n", s - 1))
            if s < LAST:
                weave_dh_on_gpsimd(s)
            else:
                weave_on_vector(new_packed(("dh_n", s)), dh[s][:].rearrange("p (b t) j -> p b t j", b=1))
            for args in todo[2:]:
                dx_bank(*args)
            if s in late:
                turn(late[s])
                unquantised = [late[s]] + unquantised
            if s < LAST:
                weave_dh_on_scalar(s)
            for load, index in loads.get(s, []):
                load(index)

        rest = dx_banks[DX_PER_STEP * (len(TILES) - FIRST_DX) :]
        for args in rest[:DX_PER_STEP]:
            dx_bank(*args)
        turn_dh(LAST)
        quantise(("dh_m", LAST - 1))
        quantise(("dh_n", LAST))
        weave_x(0)
        for args in rest[DX_PER_STEP:]:
            dx_bank(*args)
        quantise(("dh_m", LAST))
        quantise(("x", 0))
        weave_x(1)

        slices = K // P
        for j in range(slices):
            dw_bank(0, j)
            if j + 1 < slices:
                quantise(("x", j + 1))
            if j + 2 < slices:
                weave_x(j + 2)
            dw_bank(1, j, on_scalar if j + 2 < slices else on_vector)
